import numpy as np
CORES = [0,1,2,3]
N = 4
ROOT = 0
def setup_inputs(rng):
    return {"x": rng.standard_normal((N, 128, N * 4), dtype=np.float32)}
def reference(x):
    return {"y": np.stack([x[ROOT][:, r * 4:(r + 1) * 4] for r in range(N)])}

@@ -1,0 +1,40 @@
+from concourse.bass import DstId, RemoteDMATransfer
+
+BLK = 4
+ENG = 4
+
+SCRATCH = {
+    "stage": ("sbuf", [128, 12], "float32"),
+    "land": ("dram", [128, 4], "float32"),
+}
+SEMAPHORES = ["loaded", "own", "sent", "arrived", "stored"]
+
+
+def rank_program(g, core, T, topo):
+    rank = T.rank_of(core)
+    if rank is None:
+        return
+    n = len(T.cores)
+
+    if rank == 0:
+        g.scalar.dma_start(T.y[:, :], T.x[:, 0:BLK]).then_inc(T.sem.own, 16)
+        g.sync.dma_start(T.stage[:, :], T.x[:, BLK:n * BLK]).then_inc(T.sem.loaded, 16)
+        g.wait_ge(T.sem.loaded, 16)
+        transfers = []
+        for r in range(1, n):
+            dst = T.cores[r]
+            rid, pid, _se = topo.addr(dst)
+            transfers.append(RemoteDMATransfer(
+                dst_ids=[DstId(rid=rid, pnc=pid)],
+                dma_engine_mask=((1 << ENG) - 1) << (ENG * (r - 1)),
+                remote_sem=T.sem.arrived,
+                src=T.stage[:, (r - 1) * BLK:r * BLK],
+                dst=T.land[:, :],
+            ))
+        g.remote_dma_fused(transfers, local_sem=T.sem.sent)
+        g.wait_ge(T.sem.sent, ENG * (n - 1))
+        g.wait_ge(T.sem.own, 16)
+    else:
+        g.sync.wait_ge(T.sem.arrived, ENG)
+        g.sync.dma_start(T.y[:, :], T.land[:, :]).then_inc(T.sem.stored, 16)
+        g.wait_ge(T.sem.stored, 16)

@@ -4,10 +4,10 @@ BLK = 4
 ENG = 4
 
 SCRATCH = {
-    "stage": ("sbuf", [128, 12], "float32"),
+    "stage": ("dram", [3, 128, 4], "float32"),
     "land": ("dram", [128, 4], "float32"),
 }
-SEMAPHORES = ["loaded", "own", "sent", "arrived", "stored"]
+SEMAPHORES = ["packed", "own", "sent", "arrived", "stored"]
 
 
 def rank_program(g, core, T, topo):
@@ -17,18 +17,20 @@ def rank_program(g, core, T, topo):
     n = len(T.cores)
 
     if rank == 0:
+        queues = [g.sync, g.scalar]
+        for r in range(1, n):
+            q = queues[(r - 1) % 2]
+            q.dma_start(T.stage[r - 1], T.x[:, r * BLK:(r + 1) * BLK]).then_inc(T.sem.packed, 16)
         g.scalar.dma_start(T.y[:, :], T.x[:, 0:BLK]).then_inc(T.sem.own, 16)
-        g.sync.dma_start(T.stage[:, :], T.x[:, BLK:n * BLK]).then_inc(T.sem.loaded, 16)
-        g.wait_ge(T.sem.loaded, 16)
+        g.wait_ge(T.sem.packed, 16 * (n - 1))
         transfers = []
         for r in range(1, n):
-            dst = T.cores[r]
-            rid, pid, _se = topo.addr(dst)
+            rid, pid, _se = topo.addr(T.cores[r])
             transfers.append(RemoteDMATransfer(
                 dst_ids=[DstId(rid=rid, pnc=pid)],
                 dma_engine_mask=((1 << ENG) - 1) << (ENG * (r - 1)),
                 remote_sem=T.sem.arrived,
-                src=T.stage[:, (r - 1) * BLK:r * BLK],
+                src=T.stage[r - 1],
                 dst=T.land[:, :],
             ))
         g.remote_dma_fused(transfers, local_sem=T.sem.sent)

from concourse.bass import DstId, RemoteDMATransfer

BLK = 4
ENG = 4

SCRATCH = {
    "stage": ("dram", [3, 128, 4], "float32"),
    "land": ("dram", [128, 4], "float32"),
}
SEMAPHORES = ["packed", "own", "sent", "arrived", "stored"]


def rank_program(g, core, T, topo):
    rank = T.rank_of(core)
    if rank is None:
        return
    n = len(T.cores)

    if rank == 0:
        queues = [g.sync, g.scalar]
        for r in range(1, n):
            q = queues[(r - 1) % 2]
            q.dma_start(T.stage[r - 1], T.x[:, r * BLK:(r + 1) * BLK]).then_inc(T.sem.packed, 16)
        g.scalar.dma_start(T.y[:, :], T.x[:, 0:BLK]).then_inc(T.sem.own, 16)
        g.wait_ge(T.sem.packed, 16 * (n - 1))
        transfers = []
        for r in range(1, n):
            rid, pid, _se = topo.addr(T.cores[r])
            transfers.append(RemoteDMATransfer(
                dst_ids=[DstId(rid=rid, pnc=pid)],
                dma_engine_mask=((1 << ENG) - 1) << (ENG * (r - 1)),
                remote_sem=T.sem.arrived,
                src=T.stage[r - 1],
                dst=T.land[:, :],
            ))
        g.remote_dma_fused(transfers, local_sem=T.sem.sent)
        g.wait_ge(T.sem.sent, ENG * (n - 1))
        g.wait_ge(T.sem.own, 16)
    else:
        g.sync.wait_ge(T.sem.arrived, ENG)
        g.sync.dma_start(T.y[:, :], T.land[:, :]).then_inc(T.sem.stored, 16)
        g.wait_ge(T.sem.stored, 16)
